import numpy as np
import ml_dtypes


def mxq(x, axis, fmt="e4m3"):
    dtype, down = {"e4m3": (ml_dtypes.float8_e4m3fn, 7), "e5m2": (ml_dtypes.float8_e5m2, 14)}[fmt]
    v = np.moveaxis(np.asarray(x, np.float32).astype(ml_dtypes.bfloat16).astype(np.float64), axis, -1)
    blocks = v.reshape(v.shape[:-1] + (-1, 32))
    amax = np.abs(blocks).max(-1, keepdims=True)
    byte = np.maximum(np.where(amax > 0, np.frexp(amax)[1] - 1 + 127, 0) - down, 1)
    scale = np.exp2(byte - 127.0)
    codes = (blocks / scale).astype(np.float32).astype(dtype).astype(np.float64)
    return np.moveaxis((codes * scale).reshape(v.shape), -1, axis)


WIDE = False


def mx_kscale(k):
    if not WIDE:
        return np.ones(k)
    levels = np.array([10, -10, 5, -5, 0])
    if k % 512:
        return np.exp2(np.random.permutation(np.resize(levels, k // 32))).repeat(32)
    a = np.empty((k // 512, 16))
    for p in range(k // 512):
        a[p, :8] = np.random.permutation(np.resize(levels, 8))
        for g in range(8):
            far = levels[np.abs(levels - a[p, g]) >= 10]
            a[p, g + 8] = far[np.random.randint(len(far))]
    return np.exp2(a.ravel()).repeat(32)


def f64(x):
    return np.asarray(x).astype(np.float64)


def striped(idx):
    return np.tile(idx.reshape(-1, 16).T, (8, 1)).astype(np.uint16)


def unstriped(offs):
    return offs[:16].T.reshape(-1).astype(np.int64)


E2M1 = np.array([0.0, 0.5, 1.0, 1.5, 2.0, 3.0, 4.0, 6.0, -0.0, -0.5, -1.0, -1.5, -2.0, -3.0, -4.0, -6.0])


def pack_weight(w, fmt):
    k, n = w.shape
    w = f64(np.asarray(w, np.float32).astype(ml_dtypes.bfloat16)).reshape(k // 32, 32, n)
    amax = np.abs(w).max(1)
    if fmt == "e4m3":
        byte = np.frexp(amax)[1] - 1 + 127 - 7
    else:
        mant, ex = np.frexp(amax / 6.0)
        byte = np.where(mant > 0.5, ex, ex - 1) + 127
    byte = np.clip(np.where(amax > 0, byte, 1), 1, 254)
    scaled = (w * np.exp2(127.0 - byte)[:, None, :]).reshape(k, n).astype(np.float32)
    by_word = np.ascontiguousarray(scaled.reshape(k // 512, 128, 4, n).transpose(0, 1, 3, 2))
    if fmt == "e4m3":
        words = by_word.astype(ml_dtypes.float8_e4m3fn).view(np.uint8)
    else:
        c = by_word.astype(ml_dtypes.float4_e2m1fn).view(np.uint8) & 0xF
        words = (c[..., 0::2] | (c[..., 1::2] << 4)).reshape(k // 512, 128, 2 * n)
    return np.ascontiguousarray(words), np.ascontiguousarray(byte.astype(np.uint8).reshape(k // 512, 16, n))


def unpack_weight(words, scales, fmt):
    g, _, n = scales.shape
    words = np.ascontiguousarray(words).reshape(g, 128, n, -1)
    if fmt == "e4m3":
        vals = words.view(ml_dtypes.float8_e4m3fn).astype(np.float64)
    else:
        nib = np.empty((g, 128, n, 4), np.uint8)
        nib[..., 0::2] = words & 0xF
        nib[..., 1::2] = words >> 4
        vals = E2M1[nib]
    vals = vals * np.repeat(np.exp2(scales.astype(np.float64) - 127.0), 8, axis=1)[..., None]
    return vals.transpose(0, 1, 3, 2).reshape(g * 512, n)


def relu2(v):
    return np.maximum(v, 0.0) ** 2


K, T, E, C, H, N = 1024, 512, 4, 256, 512, 384


def by_expert(wq, xq):
    return np.concatenate([wq[e].T @ xq[:, e * C:(e + 1) * C] for e in range(E)], axis=1)


def setup_inputs():
    n = np.random.standard_normal
    s = mx_kscale(K)[:, None]
    u = mx_kscale(H)
    first = np.random.permutation(np.repeat(np.arange(E), T // E))
    second = (first + 1 + np.random.permutation(np.repeat(np.arange(E - 1), -(-T // (E - 1)))[:T])) % E
    while np.bincount(second, minlength=E).max() != T // E:
        load = np.bincount(second, minlength=E); hi, lo = int(load.argmax()), int(load.argmin())
        t = np.flatnonzero((second == hi) & (first != lo))[0]; second[t] = lo
    slot_token = np.empty(E * C, np.int64); pos = np.empty((2, T), np.int64); fill = np.zeros(E, np.int64)
    place = np.stack([np.random.permutation(C) for _ in range(E)])
    for r, deal in enumerate((first, second)):
        for t in np.random.permutation(T):
            e = deal[t]; j = e * C + place[e, fill[e]]; fill[e] += 1; slot_token[j] = t; pos[r, t] = j
    g = np.random.uniform(0.2, 0.8, T)
    w1 = [pack_weight(m, "e2m1") for m in n((E + 1, K, H)) / np.sqrt(K) / s[None] * u[None, None, :]]
    w2 = [pack_weight(m, "e2m1") for m in n((E + 1, H, N)) / np.sqrt(H) / u[None, :, None] ** 2]
    return {
        "xT": (n((K, T)) * s).astype(np.float32),
        "w1_words": np.stack([m[0] for m in w1]),
        "w1_scales": np.stack([m[1] for m in w1]),
        "w2_words": np.stack([m[0] for m in w2]),
        "w2_scales": np.stack([m[1] for m in w2]),
        "gate": np.stack([np.tile(g, (N, 1)), np.tile(1.0 - g, (N, 1))]).astype(np.float32),
        "offs": striped(slot_token),
        "pos1": striped(pos[0]),
        "pos2": striped(pos[1]),
    }


def reference(xT, w1_words, w1_scales, w2_words, w2_scales, gate, offs, pos1, pos2):
    idx = unstriped(offs)
    w1 = np.stack([unpack_weight(w1_words[e], w1_scales[e], "e2m1") for e in range(E + 1)])
    w2 = np.stack([unpack_weight(w2_words[e], w2_scales[e], "e2m1") for e in range(E + 1)])
    w1q, w2q = w1, w2
    xs = mxq(f64(xT), 0, "e4m3")
    hs = relu2(w1q[E].T @ xs)
    ys = w2q[E].T @ mxq(hs, 0, "e4m3")
    xq = mxq(f64(xT)[:, idx], 0, "e4m3")
    h = relu2(by_expert(w1q, xq))
    y = by_expert(w2q, mxq(h, 0, "e4m3"))
    return ys + f64(gate[0]) * y[:, unstriped(pos1)] + f64(gate[1]) * y[:, unstriped(pos2)]

@@ -1,0 +1,269 @@
+from contextlib import ExitStack
+
+import concourse.mybir as mybir
+from concourse.masks import make_identity
+
+K, T, E, C, H, N = 1024, 512, 4, 256, 512, 384
+FLOPS = 2 * (E * C + T) * H * (K + N)
+
+F32 = mybir.dt.float32
+BF16 = mybir.dt.bfloat16
+I32 = mybir.dt.int32
+U32 = mybir.dt.uint32
+U16 = mybir.dt.uint16
+U8 = mybir.dt.uint8
+FP8X4 = mybir.dt.float8_e4m3fn_x4
+FP4X4 = mybir.dt.float4_e2m1fn_x4
+RELU = mybir.ActivationFunctionType.Relu
+SQUARE = mybir.ActivationFunctionType.Square
+COPY = mybir.ActivationFunctionType.Copy
+MULT = mybir.AluOpType.mult
+ADD = mybir.AluOpType.add
+
+P = 128
+S = K // 512
+NC = N // P
+
+
+def tile_moe_shr_mlp_relu2_kernel(
+    tc, xT, w1_words, w1_scales, w2_words, w2_scales, gate, offs, pos1, pos2, out
+):
+    nc = tc.nc
+    with ExitStack() as ctx:
+        keep = ctx.enter_context(tc.tile_pool(name="keep", bufs=1))
+        work = ctx.enter_context(tc.tile_pool(name="work", bufs=3))
+        pa = ctx.enter_context(tc.psum_pool(name="pa", bufs=3))
+        pt = ctx.enter_context(tc.psum_pool(name="pt", bufs=3))
+        py = ctx.enter_context(tc.psum_pool(name="py", bufs=2))
+
+        offs_sb = keep.tile([P, E * C // 16], U16, name="offs_sb")
+        pos_sb = [keep.tile([P, T // 16], U16, name=f"pos_sb{r}") for r in range(2)]
+        ident = keep.tile([P, P], F32, name="ident")
+        x = [keep.tile([P, 4, T], F32, name=f"x{s}") for s in range(S)]
+        pairs = keep.tile([P, 2 * S, 2 * T], BF16, name="pairs", align_bytes=64)
+        w1 = keep.tile([P, (E + 1) * S, 2 * H], U8, name="w1", align_bytes=64)
+        w1s = keep.tile([P, (E + 1) * S, H], U8, name="w1s", align_bytes=64)
+        w2 = keep.tile([P, E + 1, 2 * N], U8, name="w2", align_bytes=64)
+        w2s = keep.tile([P, E + 1, N], U8, name="w2s", align_bytes=64)
+        gt = keep.tile([P, 2, NC, T], F32, name="gt")
+        y = [keep.tile([P, E * C], F32, name=f"y{c}") for c in range(NC)]
+        warm = keep.tile([P, 1], F32, name="warm")
+
+        nc.vector.memset(warm[:], 0.0)
+        nc.scalar.activation(warm[:], warm[:], RELU)
+        nc.gpsimd.memset(w1s[:].bitcast(I32), 0)
+        nc.gpsimd.memset(w2s[:].bitcast(I32), 0)
+        make_identity(nc, ident[:])
+
+        xv = xT.rearrange("(s p d) t -> s p d t", s=S, d=4)
+        nc.sync.dma_start(offs_sb[:], offs)
+        for s in range(S):
+            for u in range(2):
+                nc.sync.dma_start(out=x[s][:, 2 * u : 2 * u + 2, :], in_=xv[s, :, 2 * u : 2 * u + 2, :])
+        sv1 = w1_scales.rearrange("e s (q r) i -> q r (e s) i", q=4)
+        sv2 = w2_scales.rearrange("e s (q r) i -> q r (e s) i", q=4)
+        for q in range(4):
+            nc.sync.dma_start(out=w1s[32 * q : 32 * q + 4, :, :].bitcast(I32), in_=sv1[q].bitcast(I32))
+        order = [E, 0, 1, 2, 3]
+        for e in order[:2]:
+            nc.sync.dma_start(out=w1[:, S * e : S * e + S, :].bitcast(I32), in_=w1_words[e].rearrange("s p b -> p s b").bitcast(I32))
+        for q in range(4):
+            nc.sync.dma_start(out=w2s[32 * q : 32 * q + 4, :, :].bitcast(I32), in_=sv2[q].bitcast(I32))
+        for e in order[2:]:
+            nc.sync.dma_start(out=w1[:, S * e : S * e + S, :].bitcast(I32), in_=w1_words[e].rearrange("s p b -> p s b").bitcast(I32))
+        nc.sync.dma_start(out=w2[:].bitcast(I32), in_=w2_words.rearrange("e s p b -> p (e s) b").bitcast(I32))
+        for r, lst in enumerate((pos1, pos2)):
+            nc.sync.dma_start(pos_sb[r][:], lst)
+        for c in range(NC):
+            nc.sync.dma_start(out=gt[:, :, c, :], in_=gate.rearrange("g (c p) t -> c p g t", p=P)[c])
+
+        xs = [keep.tile([P, 4 * T], BF16, name=f"xs{s}", align_bytes=64) for s in range(S)]
+        sc = keep.tile([P, S, T], U32, name="sc", align_bytes=64)
+        ss = keep.tile([P, S, T], U8, name="ss", align_bytes=64)
+        hc = keep.tile([P, T], U32, name="hc", align_bytes=64)
+        hss = keep.tile([P, T], U8, name="hss", align_bytes=64)
+
+        def cast_pairs(j):
+            s, u = divmod(j, 2)
+            dst = pairs[:, j, :].rearrange("p (t d) -> p t d", d=2)
+            src = x[s][:, 2 * u : 2 * u + 2, :].rearrange("p d t -> p t d")
+            if j in (0, 3):
+                nc.vector.tensor_copy(out=dst, in_=src)
+            else:
+                nc.scalar.activation(dst, src, COPY)
+
+        def cast_shared(s, half):
+            cols = slice(C * half, C * (half + 1))
+            nc.scalar.activation(
+                xs[s][:].rearrange("p (t d) -> p t d", d=4)[:, cols, :], x[s][:, :, cols].rearrange("p d t -> p t d"), COPY
+            )
+
+        def new_gathered():
+            return work.tile([P, 2 * S, 2 * C], BF16, name="g", align_bytes=64, bufs=2)
+
+        def gather(e, g, j):
+            nc.vector.tensor_copy(
+                g[:, j, :].bitcast(U32),
+                pairs[:, j, :].bitcast(U32).indirect(offs_sb[:, e * C // 16 : (e + 1) * C // 16]),
+            )
+
+        def new_codes():
+            gi = work.tile([P, S, 4 * C], BF16, name="gi", align_bytes=64)
+            xc = work.tile([P, S, C], U32, name="xc", align_bytes=64)
+            xsc = work.tile([P, S, C], U8, name="xsc", align_bytes=64)
+            return gi, xc, xsc
+
+        def interleave(g, gi, s0, s1):
+            nc.vector.tensor_copy(
+                out=gi[:, s0:s1, :].bitcast(I32).rearrange("p s (c u) -> p s c u", u=2),
+                in_=g[:, 2 * s0 : 2 * s1, :].bitcast(I32).rearrange("p (s u) c -> p s c u", u=2),
+            )
+
+        def quantize(gi, xc, xsc, s0, s1):
+            nc.vector.quantize_mx(
+                out=xc[:, s0:s1, :].rearrange("p s c -> p (s c)").bitcast(FP8X4),
+                scales=xsc[:, s0:s1, :].rearrange("p s c -> p (s c)"),
+                in_=gi[:, s0:s1, :].rearrange("p s c -> p (s c)"),
+            )
+
+        def layer1(e, xc, xsc, c0, vector_tiles):
+            rs = []
+            accs = [pa.tile([P, H], F32, name="a") for m in range(2)]
+            for m in range(2):
+                cols = slice(c0 + P * m, c0 + P * (m + 1))
+                for s in range(S):
+                    nc.tensor.matmul_mx(
+                        out=accs[m][:],
+                        lhsT=xc[:, s, cols].bitcast(FP8X4),
+                        lhsT_scale=xsc[:, s, cols],
+                        rhs=w1[:, S * e + s, :].bitcast(FP4X4),
+                        rhs_scale=w1s[:, S * e + s, :],
+                        start=(s == 0),
+                        stop=(s == S - 1),
+                    )
+            for m in range(2):
+                r = work.tile([P, 4, P], F32, name="r", bufs=8)
+                acc = accs[m][:].rearrange("m (p t) -> m t p", t=4)
+                if m in vector_tiles:
+                    nc.vector.tensor_scalar(r[:], acc, 0.0, None, mybir.AluOpType.max)
+                else:
+                    nc.scalar.activation(r[:], acc, RELU)
+                rs.append(r)
+            return rs
+
+        def turn(rs):
+            hi = work.tile([P, 2, 4 * P], BF16, name="hi", align_bytes=64)
+            for m in range(2):
+                tp = pt.tile([P, 4, P], F32, name="tp")
+                for t in range(4):
+                    nc.tensor.transpose(tp[:, t, :], rs[m][:, t, :], ident[:])
+                nc.scalar.activation(hi[:, m, :].rearrange("p (r t) -> p r t", t=4), tp[:].rearrange("p t r -> p r t"), SQUARE)
+            return hi
+
+        def quantize_h(hi, hq, hs):
+            nc.vector.quantize_mx(out=hq.bitcast(FP8X4), scales=hs, in_=hi[:].rearrange("p m c -> p (m c)"))
+
+        def layer2(e, dst, n, hq, hs):
+            nc.tensor.matmul_mx(
+                out=dst,
+                lhsT=w2[:, e, 2 * P * n : 2 * P * (n + 1)].bitcast(FP4X4),
+                lhsT_scale=w2s[:, e, P * n : P * (n + 1)],
+                rhs=hq.bitcast(FP8X4),
+                rhs_scale=hs,
+                start=True,
+                stop=True,
+            )
+
+        def back(e, rs):
+            hi = turn(rs)
+            hq = work.tile([P, C], U32, name="hq", align_bytes=64)
+            hs = work.tile([P, C], U8, name="hs", align_bytes=64)
+            quantize_h(hi, hq[:], hs[:])
+            for n in range(NC):
+                yp = py.tile([P, C], F32, name="yp")
+                layer2(e, yp[:], n, hq[:], hs[:])
+                nc.scalar.copy(y[n][:, e * C : (e + 1) * C], yp[:])
+
+        g = [new_gathered() for e in range(2)]
+        codes = [new_codes() for e in range(2)]
+        rr = {}
+
+        def inter(e, s0, s1):
+            interleave(g[e], codes[e][0], s0, s1)
+
+        def quant(e, s0, s1):
+            quantize(codes[e][0], codes[e][1], codes[e][2], s0, s1)
+
+        def shared_quantize(s):
+            nc.vector.quantize_mx(out=sc[:, s, :].bitcast(FP8X4), scales=ss[:, s, :], in_=xs[s][:])
+
+        def first(e, vector_tiles=()):
+            rr[e] = layer1(e, codes[e][1], codes[e][2], 0, vector_tiles)
+
+        cast_pairs(0)
+        cast_pairs(1)
+        gather(0, g[0], 0)
+        gather(1, g[1], 0)
+        cast_pairs(2)
+        gather(0, g[0], 1)
+        cast_pairs(3)
+        gather(1, g[1], 1)
+        gather(0, g[0], 2)
+        gather(0, g[0], 3)
+        for s in range(S):
+            for half in range(2):
+                cast_shared(s, half)
+        gather(1, g[1], 2)
+        inter(0, 0, S)
+        gather(1, g[1], 3)
+        quant(0, 0, S)
+        first(0)
+        g.append(new_gathered())
+        codes.append(new_codes())
+        gather(2, g[2], 0)
+        inter(1, 0, S)
+        gather(2, g[2], 1)
+        quant(1, 0, S)
+        first(1)
+        gather(2, g[2], 2)
+        back(0, rr[0])
+        gather(2, g[2], 3)
+        g.append(new_gathered())
+        codes.append(new_codes())
+        gather(3, g[3], 0)
+        inter(2, 0, S)
+        gather(3, g[3], 1)
+        quant(2, 0, S)
+        first(2)
+        gather(3, g[3], 2)
+        inter(3, 0, 1)
+        back(1, rr[1])
+        gather(3, g[3], 3)
+        quant(3, 0, 1)
+        shared_quantize(0)
+        inter(3, 1, 2)
+        shared_quantize(1)
+        quant(3, 1, 2)
+        first(3, (1,))
+        back(2, rr[2])
+        back(3, rr[3])
+        for half in range(2):
+            rr[E + half] = layer1(E, sc, ss, C * half, (1,))
+        for half in range(2):
+            hi = turn(rr[E + half])
+            quantize_h(hi, hc[:, C * half : C * (half + 1)], hss[:, C * half : C * (half + 1)])
+
+        t1, t2 = [], []
+        for n in range(NC):
+            for r, ts in enumerate((t1, t2)):
+                t = keep.tile([P, T], F32, name=f"t{r}{n}")
+                nc.vector.tensor_tensor(t[:], y[n][:].indirect(pos_sb[r][:]), gt[:, r, n, :], MULT)
+                ts.append(t)
+        for n in range(NC):
+            ysp = pa.tile([P, T], F32, name="a")
+            layer2(E, ysp[:], n, hc[:], hss[:])
+            t3 = work.tile([P, T], F32, name="t3")
+            o = work.tile([P, T], F32, name="o")
+            nc.vector.tensor_tensor(t3[:], t1[n][:], ysp[:], ADD)
+            nc.vector.tensor_tensor(o[:], t2[n][:], t3[:], ADD)
+            nc.sync.dma_start(out=out[P * n : P * (n + 1), :], in_=o[:])

@@ -64,7 +64,7 @@ def tile_moe_shr_mlp_relu2_kernel(
         sv2 = w2_scales.rearrange("e s (q r) i -> q r (e s) i", q=4)
         for q in range(4):
             nc.sync.dma_start(out=w1s[32 * q : 32 * q + 4, :, :].bitcast(I32), in_=sv1[q].bitcast(I32))
-        order = [E, 0, 1, 2, 3]
+        order = [0, 1, 2, E, 3]
         for e in order[:2]:
             nc.sync.dma_start(out=w1[:, S * e : S * e + S, :].bitcast(I32), in_=w1_words[e].rearrange("s p b -> p s b").bitcast(I32))
         for q in range(4):
@@ -87,7 +87,7 @@ def tile_moe_shr_mlp_relu2_kernel(
             s, u = divmod(j, 2)
             dst = pairs[:, j, :].rearrange("p (t d) -> p t d", d=2)
             src = x[s][:, 2 * u : 2 * u + 2, :].rearrange("p d t -> p t d")
-            if j in (0, 3):
+            if j == 0:
                 nc.vector.tensor_copy(out=dst, in_=src)
             else:
                 nc.scalar.activation(dst, src, COPY)
@@ -126,42 +126,56 @@ def tile_moe_shr_mlp_relu2_kernel(
                 in_=gi[:, s0:s1, :].rearrange("p s c -> p (s c)"),
             )
 
-        def layer1(e, xc, xsc, c0, vector_tiles):
-            rs = []
-            accs = [pa.tile([P, H], F32, name="a") for m in range(2)]
-            for m in range(2):
+        def start1(k):
+            acc[k] = [pa.tile([P, H], F32, name="a") for m in range(2)]
+
+        def pass1(k, e, xc, xsc, c0, s, ms=(0, 1)):
+            for m in ms:
                 cols = slice(c0 + P * m, c0 + P * (m + 1))
-                for s in range(S):
-                    nc.tensor.matmul_mx(
-                        out=accs[m][:],
-                        lhsT=xc[:, s, cols].bitcast(FP8X4),
-                        lhsT_scale=xsc[:, s, cols],
-                        rhs=w1[:, S * e + s, :].bitcast(FP4X4),
-                        rhs_scale=w1s[:, S * e + s, :],
-                        start=(s == 0),
-                        stop=(s == S - 1),
-                    )
+                nc.tensor.matmul_mx(
+                    out=acc[k][m][:],
+                    lhsT=xc[:, s, cols].bitcast(FP8X4),
+                    lhsT_scale=xsc[:, s, cols],
+                    rhs=w1[:, S * e + s, :].bitcast(FP4X4),
+                    rhs_scale=w1s[:, S * e + s, :],
+                    start=(s == 0),
+                    stop=(s == S - 1),
+                )
+
+        def relu(k, vector_tiles=()):
+            rs[k] = []
             for m in range(2):
                 r = work.tile([P, 4, P], F32, name="r", bufs=8)
-                acc = accs[m][:].rearrange("m (p t) -> m t p", t=4)
+                src = acc[k][m][:].rearrange("m (p t) -> m t p", t=4)
                 if m in vector_tiles:
-                    nc.vector.tensor_scalar(r[:], acc, 0.0, None, mybir.AluOpType.max)
+                    nc.vector.tensor_scalar(r[:], src, 0.0, None, mybir.AluOpType.max)
                 else:
-                    nc.scalar.activation(r[:], acc, RELU)
-                rs.append(r)
-            return rs
+                    nc.scalar.activation(r[:], src, RELU)
+                rs[k].append(r)
 
-        def turn(rs):
+        def first(k, e, xc, xsc, c0, vector_tiles=()):
+            start1(k)
+            for m in range(2):
+                for s in range(S):
+                    pass1(k, e, xc, xsc, c0, s, (m,))
+            relu(k, vector_tiles)
+
+        def turn(k):
             hi = work.tile([P, 2, 4 * P], BF16, name="hi", align_bytes=64)
             for m in range(2):
                 tp = pt.tile([P, 4, P], F32, name="tp")
-                for t in range(4):
-                    nc.tensor.transpose(tp[:, t, :], rs[m][:, t, :], ident[:])
+                for q in range(4):
+                    nc.tensor.transpose(tp[:, q, :], rs[k][m][:, q, :], ident[:])
                 nc.scalar.activation(hi[:, m, :].rearrange("p (r t) -> p r t", t=4), tp[:].rearrange("p t r -> p r t"), SQUARE)
             return hi
 
         def quantize_h(hi, hq, hs):
             nc.vector.quantize_mx(out=hq.bitcast(FP8X4), scales=hs, in_=hi[:].rearrange("p m c -> p (m c)"))
+
+        def chain(e):
+            hi = turn(e)
+            hqs[e] = (work.tile([P, C], U32, name="hq", align_bytes=64, bufs=4), work.tile([P, C], U8, name="hs", align_bytes=64, bufs=4))
+            quantize_h(hi, hqs[e][0][:], hqs[e][1][:])
 
         def layer2(e, dst, n, hq, hs):
             nc.tensor.matmul_mx(
@@ -174,19 +188,29 @@ def tile_moe_shr_mlp_relu2_kernel(
                 stop=True,
             )
 
-        def back(e, rs):
-            hi = turn(rs)
-            hq = work.tile([P, C], U32, name="hq", align_bytes=64)
-            hs = work.tile([P, C], U8, name="hs", align_bytes=64)
-            quantize_h(hi, hq[:], hs[:])
-            for n in range(NC):
-                yp = py.tile([P, C], F32, name="yp")
-                layer2(e, yp[:], n, hq[:], hs[:])
-                nc.scalar.copy(y[n][:, e * C : (e + 1) * C], yp[:])
+        def results(e0, *ns):
+            for n in ns:
+                yp = py.tile([P, 2, C], F32, name="yp")
+                for e in range(e0, e0 + 2):
+                    layer2(e, yp[:, e - e0, :], n, hqs[e][0][:], hqs[e][1][:])
+                dst = y[n][:, e0 * C : (e0 + 2) * C]
+                src = yp[:].rearrange("p e c -> p (e c)")
+                if (e0, n) == (2, 0):
+                    nc.vector.tensor_copy(dst, src)
+                else:
+                    nc.scalar.copy(dst, src)
 
+        acc, rs, hqs = {}, {}, {}
         g = [new_gathered() for e in range(2)]
         codes = [new_codes() for e in range(2)]
-        rr = {}
+
+        def more():
+            g.append(new_gathered())
+            codes.append(new_codes())
+
+        def gath(e, *js):
+            for j in js:
+                gather(e, g[e], j)
 
         def inter(e, s0, s1):
             interleave(g[e], codes[e][0], s0, s1)
@@ -194,64 +218,62 @@ def tile_moe_shr_mlp_relu2_kernel(
         def quant(e, s0, s1):
             quantize(codes[e][0], codes[e][1], codes[e][2], s0, s1)
 
-        def shared_quantize(s):
-            nc.vector.quantize_mx(out=sc[:, s, :].bitcast(FP8X4), scales=ss[:, s, :], in_=xs[s][:])
+        def routed(e, vector_tiles=()):
+            first(e, e, codes[e][1], codes[e][2], 0, vector_tiles)
 
-        def first(e, vector_tiles=()):
-            rr[e] = layer1(e, codes[e][1], codes[e][2], 0, vector_tiles)
-
-        cast_pairs(0)
-        cast_pairs(1)
-        gather(0, g[0], 0)
-        gather(1, g[1], 0)
-        cast_pairs(2)
-        gather(0, g[0], 1)
-        cast_pairs(3)
-        gather(1, g[1], 1)
-        gather(0, g[0], 2)
-        gather(0, g[0], 3)
+        for j in range(2 * S):
+            cast_pairs(j)
+        gath(0, 0)
+        gath(1, 0)
+        gath(0, 1)
+        gath(1, 1)
+        gath(0, 2)
+        inter(0, 0, 1)
+        gath(0, 3)
+        quant(0, 0, 1)
+        start1(0)
+        pass1(0, 0, codes[0][1], codes[0][2], 0, 0)
+        inter(0, 1, 2)
+        gath(1, 2)
+        quant(0, 1, 2)
+        pass1(0, 0, codes[0][1], codes[0][2], 0, 1)
+        relu(0)
         for s in range(S):
             for half in range(2):
                 cast_shared(s, half)
-        gather(1, g[1], 2)
-        inter(0, 0, S)
-        gather(1, g[1], 3)
-        quant(0, 0, S)
-        first(0)
-        g.append(new_gathered())
-        codes.append(new_codes())
-        gather(2, g[2], 0)
-        inter(1, 0, S)
-        gather(2, g[2], 1)
-        quant(1, 0, S)
-        first(1)
-        gather(2, g[2], 2)
-        back(0, rr[0])
-        gather(2, g[2], 3)
-        g.append(new_gathered())
-        codes.append(new_codes())
-        gather(3, g[3], 0)
-        inter(2, 0, S)
-        gather(3, g[3], 1)
-        quant(2, 0, S)
-        first(2)
-        gather(3, g[3], 2)
-        inter(3, 0, 1)
-        back(1, rr[1])
-        gather(3, g[3], 3)
-        quant(3, 0, 1)
-        shared_quantize(0)
-        inter(3, 1, 2)
-        shared_quantize(1)
-        quant(3, 1, 2)
-        first(3, (1,))
-        back(2, rr[2])
-        back(3, rr[3])
+        gath(1, 3)
+        inter(1, 0, 2)
+        more()
+        gath(2, 0)
+        quant(1, 0, 2)
+        routed(1)
+        gath(2, 1, 2)
+        chain(0)
+        gath(2, 3)
+        more()
+        gath(3, 0)
+        inter(2, 0, 2)
+        gath(3, 1)
+        quant(2, 0, 2)
+        routed(2)
+        gath(3, 2, 3)
+        chain(1)
+        inter(3, 0, 2)
+        quant(3, 0, 2)
+        routed(3, (0,))
+        for s in range(S):
+            nc.vector.quantize_mx(out=sc[:, s, :].bitcast(FP8X4), scales=ss[:, s, :], in_=xs[s][:])
+        chain(2)
+        chain(3)
+        results(0, 0, 1)
+        results(2, 0, 1)
         for half in range(2):
-            rr[E + half] = layer1(E, sc, ss, C * half, (1,))
+            first(E + half, E, sc, ss, C * half)
         for half in range(2):
-            hi = turn(rr[E + half])
+            hi = turn(E + half)
             quantize_h(hi, hc[:, C * half : C * (half + 1)], hss[:, C * half : C * (half + 1)])
+        results(0, 2)
+        results(2, 2)
 
         t1, t2 = [], []
         for n in range(NC):
@@ -259,11 +281,24 @@ def tile_moe_shr_mlp_relu2_kernel(
                 t = keep.tile([P, T], F32, name=f"t{r}{n}")
                 nc.vector.tensor_tensor(t[:], y[n][:].indirect(pos_sb[r][:]), gt[:, r, n, :], MULT)
                 ts.append(t)
+        ysp = []
         for n in range(NC):
-            ysp = pa.tile([P, T], F32, name="a")
-            layer2(E, ysp[:], n, hc[:], hss[:])
-            t3 = work.tile([P, T], F32, name="t3")
-            o = work.tile([P, T], F32, name="o")
-            nc.vector.tensor_tensor(t3[:], t1[n][:], ysp[:], ADD)
-            nc.vector.tensor_tensor(o[:], t2[n][:], t3[:], ADD)
-            nc.sync.dma_start(out=out[P * n : P * (n + 1), :], in_=o[:])
+            ysp.append(pa.tile([P, T], F32, name="a"))
+            layer2(E, ysp[n][:], n, hc[:], hss[:])
+        t3 = [keep.tile([P, T], F32, name=f"t3{n}") for n in range(NC)]
+        o = [keep.tile([P, T], F32, name=f"o{n}") for n in range(NC)]
+
+        def plus_shared(n):
+            nc.vector.tensor_tensor(t3[n][:], t1[n][:], ysp[n][:], ADD)
+
+        def finish(n, c0, c1):
+            nc.vector.tensor_tensor(o[n][:, c0:c1], t2[n][:, c0:c1], t3[n][:, c0:c1], ADD)
+            nc.sync.dma_start(out=out[P * n : P * (n + 1), c0:c1], in_=o[n][:, c0:c1])
+
+        plus_shared(0)
+        plus_shared(1)
+        finish(0, 0, T)
+        plus_shared(2)
+        finish(1, 0, T)
+        finish(2, 0, T // 2)
+        finish(2, T // 2, T)

@@ -56,10 +56,11 @@ def tile_moe_shr_mlp_relu2_kernel(
         make_identity(nc, ident[:])
 
         xv = xT.rearrange("(s p d) t -> s p d t", s=S, d=4)
-        nc.sync.dma_start(offs_sb[:], offs)
         for s in range(S):
             for u in range(2):
                 nc.sync.dma_start(out=x[s][:, 2 * u : 2 * u + 2, :], in_=xv[s, :, 2 * u : 2 * u + 2, :])
+                if s == 0 and u == 0:
+                    nc.sync.dma_start(offs_sb[:], offs)
         sv1 = w1_scales.rearrange("e s (q r) i -> q r (e s) i", q=4)
         sv2 = w2_scales.rearrange("e s (q r) i -> q r (e s) i", q=4)
         for q in range(4):
@@ -78,8 +79,6 @@ def tile_moe_shr_mlp_relu2_kernel(
             nc.sync.dma_start(out=gt[:, :, c, :], in_=gate.rearrange("g (c p) t -> c p g t", p=P)[c])
 
         xs = [keep.tile([P, 4 * T], BF16, name=f"xs{s}", align_bytes=64) for s in range(S)]
-        sc = keep.tile([P, S, T], U32, name="sc", align_bytes=64)
-        ss = keep.tile([P, S, T], U8, name="ss", align_bytes=64)
         hc = keep.tile([P, T], U32, name="hc", align_bytes=64)
         hss = keep.tile([P, T], U8, name="hss", align_bytes=64)
 
@@ -94,9 +93,12 @@ def tile_moe_shr_mlp_relu2_kernel(
 
         def cast_shared(s, half):
             cols = slice(C * half, C * (half + 1))
-            nc.scalar.activation(
-                xs[s][:].rearrange("p (t d) -> p t d", d=4)[:, cols, :], x[s][:, :, cols].rearrange("p d t -> p t d"), COPY
-            )
+            dst = xs[s][:].rearrange("p (t d) -> p t d", d=4)[:, cols, :]
+            src = x[s][:, :, cols].rearrange("p d t -> p t d")
+            if s == 0:
+                nc.gpsimd.tensor_scalar(dst, src, 1.0, 0.0, MULT, ADD)
+            else:
+                nc.scalar.activation(dst, src, COPY)
 
         def new_gathered():
             return work.tile([P, 2 * S, 2 * C], BF16, name="g", align_bytes=64, bufs=2)
@@ -108,7 +110,7 @@ def tile_moe_shr_mlp_relu2_kernel(
             )
 
         def new_codes():
-            gi = work.tile([P, S, 4 * C], BF16, name="gi", align_bytes=64)
+            gi = work.tile([P, S, 4 * C], BF16, name="gi", align_bytes=64, bufs=1)
             xc = work.tile([P, S, C], U32, name="xc", align_bytes=64)
             xsc = work.tile([P, S, C], U8, name="xsc", align_bytes=64)
             return gi, xc, xsc
@@ -160,22 +162,21 @@ def tile_moe_shr_mlp_relu2_kernel(
                     pass1(k, e, xc, xsc, c0, s, (m,))
             relu(k, vector_tiles)
 
-        def turn(k):
-            hi = work.tile([P, 2, 4 * P], BF16, name="hi", align_bytes=64)
+        def turn(k, hi):
             for m in range(2):
                 tp = pt.tile([P, 4, P], F32, name="tp")
                 for q in range(4):
                     nc.tensor.transpose(tp[:, q, :], rs[k][m][:, q, :], ident[:])
                 nc.scalar.activation(hi[:, m, :].rearrange("p (r t) -> p r t", t=4), tp[:].rearrange("p t r -> p r t"), SQUARE)
-            return hi
 
         def quantize_h(hi, hq, hs):
-            nc.vector.quantize_mx(out=hq.bitcast(FP8X4), scales=hs, in_=hi[:].rearrange("p m c -> p (m c)"))
+            nc.vector.quantize_mx(out=hq.bitcast(FP8X4), scales=hs, in_=hi.rearrange("p m c -> p (m c)"))
 
         def chain(e):
-            hi = turn(e)
+            hi = work.tile([P, 2, 4 * P], BF16, name="hi", align_bytes=64)
+            turn(e, hi[:])
             hqs[e] = (work.tile([P, C], U32, name="hq", align_bytes=64, bufs=4), work.tile([P, C], U8, name="hs", align_bytes=64, bufs=4))
-            quantize_h(hi, hqs[e][0][:], hqs[e][1][:])
+            quantize_h(hi[:], hqs[e][0][:], hqs[e][1][:])
 
         def layer2(e, dst, n, hq, hs):
             nc.tensor.matmul_mx(
@@ -202,17 +203,18 @@ def tile_moe_shr_mlp_relu2_kernel(
 
         acc, rs, hqs = {}, {}, {}
         g = [new_gathered() for e in range(2)]
-        codes = [new_codes() for e in range(2)]
+        codes = []
 
         def more():
             g.append(new_gathered())
-            codes.append(new_codes())
 
         def gath(e, *js):
             for j in js:
                 gather(e, g[e], j)
 
         def inter(e, s0, s1):
+            if e == len(codes):
+                codes.append(new_codes())
             interleave(g[e], codes[e][0], s0, s1)
 
         def quant(e, s0, s1):
@@ -227,21 +229,21 @@ def tile_moe_shr_mlp_relu2_kernel(
         gath(1, 0)
         gath(0, 1)
         gath(1, 1)
-        gath(0, 2)
         inter(0, 0, 1)
-        gath(0, 3)
+        gath(0, 2)
         quant(0, 0, 1)
         start1(0)
         pass1(0, 0, codes[0][1], codes[0][2], 0, 0)
-        inter(0, 1, 2)
+        gath(0, 3)
         gath(1, 2)
+        inter(0, 1, 2)
+        gath(1, 3)
         quant(0, 1, 2)
         pass1(0, 0, codes[0][1], codes[0][2], 0, 1)
         relu(0)
         for s in range(S):
             for half in range(2):
                 cast_shared(s, half)
-        gath(1, 3)
         inter(1, 0, 2)
         more()
         gath(2, 0)
@@ -250,17 +252,18 @@ def tile_moe_shr_mlp_relu2_kernel(
         gath(2, 1, 2)
         chain(0)
         gath(2, 3)
+        inter(2, 0, 2)
         more()
         gath(3, 0)
-        inter(2, 0, 2)
-        gath(3, 1)
         quant(2, 0, 2)
         routed(2)
-        gath(3, 2, 3)
+        gath(3, 1, 2, 3)
         chain(1)
         inter(3, 0, 2)
         quant(3, 0, 2)
         routed(3, (0,))
+        sc = work.tile([P, S, T], U32, name="gi", align_bytes=64, bufs=1)
+        ss = keep.tile([P, S, T], U8, name="ss", align_bytes=64)
         for s in range(S):
             nc.vector.quantize_mx(out=sc[:, s, :].bitcast(FP8X4), scales=ss[:, s, :], in_=xs[s][:])
         chain(2)
@@ -269,9 +272,10 @@ def tile_moe_shr_mlp_relu2_kernel(
         results(2, 0, 1)
         for half in range(2):
             first(E + half, E, sc, ss, C * half)
+        hsi = keep.tile([P, 4, 4 * P], BF16, name="hsi", align_bytes=64)
         for half in range(2):
-            hi = turn(E + half)
-            quantize_h(hi, hc[:, C * half : C * (half + 1)], hss[:, C * half : C * (half + 1)])
+            turn(E + half, hsi[:, 2 * half : 2 * half + 2, :])
+        quantize_h(hsi[:], hc[:], hss[:])
         results(0, 2)
         results(2, 2)
 
@@ -291,14 +295,14 @@ def tile_moe_shr_mlp_relu2_kernel(
         def plus_shared(n):
             nc.vector.tensor_tensor(t3[n][:], t1[n][:], ysp[n][:], ADD)
 
-        def finish(n, c0, c1):
-            nc.vector.tensor_tensor(o[n][:, c0:c1], t2[n][:, c0:c1], t3[n][:, c0:c1], ADD)
+        def finish(n, c0, c1, engine):
+            engine.tensor_tensor(o[n][:, c0:c1], t2[n][:, c0:c1], t3[n][:, c0:c1], ADD)
             nc.sync.dma_start(out=out[P * n : P * (n + 1), c0:c1], in_=o[n][:, c0:c1])
 
         plus_shared(0)
+        finish(0, 0, T, nc.gpsimd)
         plus_shared(1)
-        finish(0, 0, T)
         plus_shared(2)
-        finish(1, 0, T)
-        finish(2, 0, T // 2)
-        finish(2, T // 2, T)
+        finish(1, 0, T, nc.vector)
+        finish(2, 0, T // 2, nc.vector)
+        finish(2, T // 2, T, nc.vector)

@@ -78,7 +78,6 @@ def tile_moe_shr_mlp_relu2_kernel(
         for c in range(NC):
             nc.sync.dma_start(out=gt[:, :, c, :], in_=gate.rearrange("g (c p) t -> c p g t", p=P)[c])
 
-        xs = [keep.tile([P, 4 * T], BF16, name=f"xs{s}", align_bytes=64) for s in range(S)]
         hc = keep.tile([P, T], U32, name="hc", align_bytes=64)
         hss = keep.tile([P, T], U8, name="hss", align_bytes=64)
 
@@ -88,15 +87,6 @@ def tile_moe_shr_mlp_relu2_kernel(
             src = x[s][:, 2 * u : 2 * u + 2, :].rearrange("p d t -> p t d")
             if j == 0:
                 nc.vector.tensor_copy(out=dst, in_=src)
-            else:
-                nc.scalar.activation(dst, src, COPY)
-
-        def cast_shared(s, half):
-            cols = slice(C * half, C * (half + 1))
-            dst = xs[s][:].rearrange("p (t d) -> p t d", d=4)[:, cols, :]
-            src = x[s][:, :, cols].rearrange("p d t -> p t d")
-            if s == 0:
-                nc.gpsimd.tensor_scalar(dst, src, 1.0, 0.0, MULT, ADD)
             else:
                 nc.scalar.activation(dst, src, COPY)
 
@@ -172,11 +162,13 @@ def tile_moe_shr_mlp_relu2_kernel(
         def quantize_h(hi, hq, hs):
             nc.vector.quantize_mx(out=hq.bitcast(FP8X4), scales=hs, in_=hi.rearrange("p m c -> p (m c)"))
 
-        def chain(e):
-            hi = work.tile([P, 2, 4 * P], BF16, name="hi", align_bytes=64)
-            turn(e, hi[:])
+        def turned(e):
+            his[e] = work.tile([P, 2, 4 * P], BF16, name="hi", align_bytes=64)
+            turn(e, his[e][:])
+
+        def hidden(e):
             hqs[e] = (work.tile([P, C], U32, name="hq", align_bytes=64, bufs=4), work.tile([P, C], U8, name="hs", align_bytes=64, bufs=4))
-            quantize_h(hi[:], hqs[e][0][:], hqs[e][1][:])
+            quantize_h(his[e][:], hqs[e][0][:], hqs[e][1][:])
 
         def layer2(e, dst, n, hq, hs):
             nc.tensor.matmul_mx(
@@ -196,12 +188,12 @@ def tile_moe_shr_mlp_relu2_kernel(
                     layer2(e, yp[:, e - e0, :], n, hqs[e][0][:], hqs[e][1][:])
                 dst = y[n][:, e0 * C : (e0 + 2) * C]
                 src = yp[:].rearrange("p e c -> p (e c)")
-                if (e0, n) == (2, 0):
+                if n == 0:
                     nc.vector.tensor_copy(dst, src)
                 else:
                     nc.scalar.copy(dst, src)
 
-        acc, rs, hqs = {}, {}, {}
+        acc, rs, his, hqs = {}, {}, {}, {}
         g = [new_gathered() for e in range(2)]
         codes = []
 
@@ -241,16 +233,13 @@ def tile_moe_shr_mlp_relu2_kernel(
         quant(0, 1, 2)
         pass1(0, 0, codes[0][1], codes[0][2], 0, 1)
         relu(0)
-        for s in range(S):
-            for half in range(2):
-                cast_shared(s, half)
         inter(1, 0, 2)
         more()
         gath(2, 0)
         quant(1, 0, 2)
         routed(1)
         gath(2, 1, 2)
-        chain(0)
+        turned(0)
         gath(2, 3)
         inter(2, 0, 2)
         more()
@@ -258,16 +247,22 @@ def tile_moe_shr_mlp_relu2_kernel(
         quant(2, 0, 2)
         routed(2)
         gath(3, 1, 2, 3)
-        chain(1)
+        turned(1)
         inter(3, 0, 2)
         quant(3, 0, 2)
-        routed(3, (0,))
-        sc = work.tile([P, S, T], U32, name="gi", align_bytes=64, bufs=1)
+        routed(3)
+        hidden(0)
+        hidden(1)
+        xs = work.tile([P, S, 4 * T], BF16, name="gi", align_bytes=64, bufs=1)
+        sc = keep.tile([P, S, T], U32, name="sc", align_bytes=64)
         ss = keep.tile([P, S, T], U8, name="ss", align_bytes=64)
         for s in range(S):
-            nc.vector.quantize_mx(out=sc[:, s, :].bitcast(FP8X4), scales=ss[:, s, :], in_=xs[s][:])
-        chain(2)
-        chain(3)
+            interleave(pairs, xs, s, s + 1)
+        for s in range(S):
+            nc.vector.quantize_mx(out=sc[:, s, :].bitcast(FP8X4), scales=ss[:, s, :], in_=xs[:, s, :])
+        for e in (2, 3):
+            turned(e)
+            hidden(e)
         results(0, 0, 1)
         results(2, 0, 1)
         for half in range(2):

@@ -105,6 +105,12 @@ def tile_moe_shr_mlp_relu2_kernel(
             xsc = work.tile([P, S, C], U8, name="xsc", align_bytes=64)
             return gi, xc, xsc
 
+        def interleave_on_scalar(g, gi, s):
+            nc.scalar.copy(
+                gi[:, s, :].rearrange("p (c u d) -> p c u d", u=2, d=2),
+                g[:, 2 * s : 2 * s + 2, :].rearrange("p u (c d) -> p c u d", d=2),
+            )
+
         def interleave(g, gi, s0, s1):
             nc.vector.tensor_copy(
                 out=gi[:, s0:s1, :].bitcast(I32).rearrange("p s (c u) -> p s c u", u=2),
@@ -188,7 +194,7 @@ def tile_moe_shr_mlp_relu2_kernel(
                     layer2(e, yp[:, e - e0, :], n, hqs[e][0][:], hqs[e][1][:])
                 dst = y[n][:, e0 * C : (e0 + 2) * C]
                 src = yp[:].rearrange("p e c -> p (e c)")
-                if n == 0:
+                if n == 0 or (e0, n) == (0, 1):
                     nc.vector.tensor_copy(dst, src)
                 else:
                     nc.scalar.copy(dst, src)
@@ -221,15 +227,14 @@ def tile_moe_shr_mlp_relu2_kernel(
         gath(1, 0)
         gath(0, 1)
         gath(1, 1)
-        inter(0, 0, 1)
-        gath(0, 2)
+        codes.append(new_codes())
+        interleave_on_scalar(g[0], codes[0][0], 0)
+        gath(0, 2, 3)
+        inter(0, 1, 2)
+        gath(1, 2, 3)
         quant(0, 0, 1)
         start1(0)
         pass1(0, 0, codes[0][1], codes[0][2], 0, 0)
-        gath(0, 3)
-        gath(1, 2)
-        inter(0, 1, 2)
-        gath(1, 3)
         quant(0, 1, 2)
         pass1(0, 0, codes[0][1], codes[0][2], 0, 1)
         relu(0)
@@ -246,11 +251,17 @@ def tile_moe_shr_mlp_relu2_kernel(
         gath(3, 0)
         quant(2, 0, 2)
         routed(2)
-        gath(3, 1, 2, 3)
+        gath(3, 1, 2)
+        inter(3, 0, 1)
+        gath(3, 3)
         turned(1)
-        inter(3, 0, 2)
-        quant(3, 0, 2)
-        routed(3)
+        quant(3, 0, 1)
+        inter(3, 1, 2)
+        quant(3, 1, 2)
+        start1(3)
+        for s in range(S):
+            pass1(3, 3, codes[3][1], codes[3][2], 0, s)
+        relu(3)
         hidden(0)
         hidden(1)
         xs = work.tile([P, S, 4 * T], BF16, name="gi", align_bytes=64, bufs=1)

from contextlib import ExitStack

import concourse.mybir as mybir
from concourse.masks import make_identity

K, T, E, C, H, N = 1024, 512, 4, 256, 512, 384
FLOPS = 2 * (E * C + T) * H * (K + N)

F32 = mybir.dt.float32
BF16 = mybir.dt.bfloat16
I32 = mybir.dt.int32
U32 = mybir.dt.uint32
U16 = mybir.dt.uint16
U8 = mybir.dt.uint8
FP8X4 = mybir.dt.float8_e4m3fn_x4
FP4X4 = mybir.dt.float4_e2m1fn_x4
RELU = mybir.ActivationFunctionType.Relu
SQUARE = mybir.ActivationFunctionType.Square
COPY = mybir.ActivationFunctionType.Copy
MULT = mybir.AluOpType.mult
ADD = mybir.AluOpType.add

P = 128
S = K // 512
NC = N // P


def tile_moe_shr_mlp_relu2_kernel(
    tc, xT, w1_words, w1_scales, w2_words, w2_scales, gate, offs, pos1, pos2, out
):
    nc = tc.nc
    with ExitStack() as ctx:
        keep = ctx.enter_context(tc.tile_pool(name="keep", bufs=1))
        work = ctx.enter_context(tc.tile_pool(name="work", bufs=3))
        pa = ctx.enter_context(tc.psum_pool(name="pa", bufs=3))
        pt = ctx.enter_context(tc.psum_pool(name="pt", bufs=3))
        py = ctx.enter_context(tc.psum_pool(name="py", bufs=2))

        offs_sb = keep.tile([P, E * C // 16], U16, name="offs_sb")
        pos_sb = [keep.tile([P, T // 16], U16, name=f"pos_sb{r}") for r in range(2)]
        ident = keep.tile([P, P], F32, name="ident")
        x = [keep.tile([P, 4, T], F32, name=f"x{s}") for s in range(S)]
        pairs = keep.tile([P, 2 * S, 2 * T], BF16, name="pairs", align_bytes=64)
        w1 = keep.tile([P, (E + 1) * S, 2 * H], U8, name="w1", align_bytes=64)
        w1s = keep.tile([P, (E + 1) * S, H], U8, name="w1s", align_bytes=64)
        w2 = keep.tile([P, E + 1, 2 * N], U8, name="w2", align_bytes=64)
        w2s = keep.tile([P, E + 1, N], U8, name="w2s", align_bytes=64)
        gt = keep.tile([P, 2, NC, T], F32, name="gt")
        y = [keep.tile([P, E * C], F32, name=f"y{c}") for c in range(NC)]
        warm = keep.tile([P, 1], F32, name="warm")

        nc.vector.memset(warm[:], 0.0)
        nc.scalar.activation(warm[:], warm[:], RELU)
        nc.gpsimd.memset(w1s[:].bitcast(I32), 0)
        nc.gpsimd.memset(w2s[:].bitcast(I32), 0)
        make_identity(nc, ident[:])

        xv = xT.rearrange("(s p d) t -> s p d t", s=S, d=4)
        for s in range(S):
            for u in range(2):
                nc.sync.dma_start(out=x[s][:, 2 * u : 2 * u + 2, :], in_=xv[s, :, 2 * u : 2 * u + 2, :])
                if s == 0 and u == 0:
                    nc.sync.dma_start(offs_sb[:], offs)
        sv1 = w1_scales.rearrange("e s (q r) i -> q r (e s) i", q=4)
        sv2 = w2_scales.rearrange("e s (q r) i -> q r (e s) i", q=4)
        for q in range(4):
            nc.sync.dma_start(out=w1s[32 * q : 32 * q + 4, :, :].bitcast(I32), in_=sv1[q].bitcast(I32))
        order = [0, 1, 2, E, 3]
        for e in order[:2]:
            nc.sync.dma_start(out=w1[:, S * e : S * e + S, :].bitcast(I32), in_=w1_words[e].rearrange("s p b -> p s b").bitcast(I32))
        for q in range(4):
            nc.sync.dma_start(out=w2s[32 * q : 32 * q + 4, :, :].bitcast(I32), in_=sv2[q].bitcast(I32))
        for e in order[2:]:
            nc.sync.dma_start(out=w1[:, S * e : S * e + S, :].bitcast(I32), in_=w1_words[e].rearrange("s p b -> p s b").bitcast(I32))
        nc.sync.dma_start(out=w2[:].bitcast(I32), in_=w2_words.rearrange("e s p b -> p (e s) b").bitcast(I32))
        for r, lst in enumerate((pos1, pos2)):
            nc.sync.dma_start(pos_sb[r][:], lst)
        for c in range(NC):
            nc.sync.dma_start(out=gt[:, :, c, :], in_=gate.rearrange("g (c p) t -> c p g t", p=P)[c])

        hc = keep.tile([P, T], U32, name="hc", align_bytes=64)
        hss = keep.tile([P, T], U8, name="hss", align_bytes=64)

        def cast_pairs(j):
            s, u = divmod(j, 2)
            dst = pairs[:, j, :].rearrange("p (t d) -> p t d", d=2)
            src = x[s][:, 2 * u : 2 * u + 2, :].rearrange("p d t -> p t d")
            if j == 0:
                nc.vector.tensor_copy(out=dst, in_=src)
            else:
                nc.scalar.activation(dst, src, COPY)

        def new_gathered():
            return work.tile([P, 2 * S, 2 * C], BF16, name="g", align_bytes=64, bufs=2)

        def gather(e, g, j):
            nc.vector.tensor_copy(
                g[:, j, :].bitcast(U32),
                pairs[:, j, :].bitcast(U32).indirect(offs_sb[:, e * C // 16 : (e + 1) * C // 16]),
            )

        def new_codes():
            gi = work.tile([P, S, 4 * C], BF16, name="gi", align_bytes=64, bufs=1)
            xc = work.tile([P, S, C], U32, name="xc", align_bytes=64)
            xsc = work.tile([P, S, C], U8, name="xsc", align_bytes=64)
            return gi, xc, xsc

        def interleave_on_scalar(g, gi, s):
            nc.scalar.copy(
                gi[:, s, :].rearrange("p (c u d) -> p c u d", u=2, d=2),
                g[:, 2 * s : 2 * s + 2, :].rearrange("p u (c d) -> p c u d", d=2),
            )

        def interleave(g, gi, s0, s1):
            nc.vector.tensor_copy(
                out=gi[:, s0:s1, :].bitcast(I32).rearrange("p s (c u) -> p s c u", u=2),
                in_=g[:, 2 * s0 : 2 * s1, :].bitcast(I32).rearrange("p (s u) c -> p s c u", u=2),
            )

        def quantize(gi, xc, xsc, s0, s1):
            nc.vector.quantize_mx(
                out=xc[:, s0:s1, :].rearrange("p s c -> p (s c)").bitcast(FP8X4),
                scales=xsc[:, s0:s1, :].rearrange("p s c -> p (s c)"),
                in_=gi[:, s0:s1, :].rearrange("p s c -> p (s c)"),
            )

        def start1(k):
            acc[k] = [pa.tile([P, H], F32, name="a") for m in range(2)]

        def pass1(k, e, xc, xsc, c0, s, ms=(0, 1)):
            for m in ms:
                cols = slice(c0 + P * m, c0 + P * (m + 1))
                nc.tensor.matmul_mx(
                    out=acc[k][m][:],
                    lhsT=xc[:, s, cols].bitcast(FP8X4),
                    lhsT_scale=xsc[:, s, cols],
                    rhs=w1[:, S * e + s, :].bitcast(FP4X4),
                    rhs_scale=w1s[:, S * e + s, :],
                    start=(s == 0),
                    stop=(s == S - 1),
                )

        def relu(k, vector_tiles=()):
            rs[k] = []
            for m in range(2):
                r = work.tile([P, 4, P], F32, name="r", bufs=8)
                src = acc[k][m][:].rearrange("m (p t) -> m t p", t=4)
                if m in vector_tiles:
                    nc.vector.tensor_scalar(r[:], src, 0.0, None, mybir.AluOpType.max)
                else:
                    nc.scalar.activation(r[:], src, RELU)
                rs[k].append(r)

        def first(k, e, xc, xsc, c0, vector_tiles=()):
            start1(k)
            for m in range(2):
                for s in range(S):
                    pass1(k, e, xc, xsc, c0, s, (m,))
            relu(k, vector_tiles)

        def turn(k, hi):
            for m in range(2):
                tp = pt.tile([P, 4, P], F32, name="tp")
                for q in range(4):
                    nc.tensor.transpose(tp[:, q, :], rs[k][m][:, q, :], ident[:])
                nc.scalar.activation(hi[:, m, :].rearrange("p (r t) -> p r t", t=4), tp[:].rearrange("p t r -> p r t"), SQUARE)

        def quantize_h(hi, hq, hs):
            nc.vector.quantize_mx(out=hq.bitcast(FP8X4), scales=hs, in_=hi.rearrange("p m c -> p (m c)"))

        def turned(e):
            his[e] = work.tile([P, 2, 4 * P], BF16, name="hi", align_bytes=64)
            turn(e, his[e][:])

        def hidden(e):
            hqs[e] = (work.tile([P, C], U32, name="hq", align_bytes=64, bufs=4), work.tile([P, C], U8, name="hs", align_bytes=64, bufs=4))
            quantize_h(his[e][:], hqs[e][0][:], hqs[e][1][:])

        def layer2(e, dst, n, hq, hs):
            nc.tensor.matmul_mx(
                out=dst,
                lhsT=w2[:, e, 2 * P * n : 2 * P * (n + 1)].bitcast(FP4X4),
                lhsT_scale=w2s[:, e, P * n : P * (n + 1)],
                rhs=hq.bitcast(FP8X4),
                rhs_scale=hs,
                start=True,
                stop=True,
            )

        def results(e0, *ns):
            for n in ns:
                yp = py.tile([P, 2, C], F32, name="yp")
                for e in range(e0, e0 + 2):
                    layer2(e, yp[:, e - e0, :], n, hqs[e][0][:], hqs[e][1][:])
                dst = y[n][:, e0 * C : (e0 + 2) * C]
                src = yp[:].rearrange("p e c -> p (e c)")
                if n == 0 or (e0, n) == (0, 1):
                    nc.vector.tensor_copy(dst, src)
                else:
                    nc.scalar.copy(dst, src)

        acc, rs, his, hqs = {}, {}, {}, {}
        g = [new_gathered() for e in range(2)]
        codes = []

        def more():
            g.append(new_gathered())

        def gath(e, *js):
            for j in js:
                gather(e, g[e], j)

        def inter(e, s0, s1):
            if e == len(codes):
                codes.append(new_codes())
            interleave(g[e], codes[e][0], s0, s1)

        def quant(e, s0, s1):
            quantize(codes[e][0], codes[e][1], codes[e][2], s0, s1)

        def routed(e, vector_tiles=()):
            first(e, e, codes[e][1], codes[e][2], 0, vector_tiles)

        for j in range(2 * S):
            cast_pairs(j)
        gath(0, 0)
        gath(1, 0)
        gath(0, 1)
        gath(1, 1)
        codes.append(new_codes())
        interleave_on_scalar(g[0], codes[0][0], 0)
        gath(0, 2, 3)
        inter(0, 1, 2)
        gath(1, 2, 3)
        quant(0, 0, 1)
        start1(0)
        pass1(0, 0, codes[0][1], codes[0][2], 0, 0)
        quant(0, 1, 2)
        pass1(0, 0, codes[0][1], codes[0][2], 0, 1)
        relu(0)
        inter(1, 0, 2)
        more()
        gath(2, 0)
        quant(1, 0, 2)
        routed(1)
        gath(2, 1, 2)
        turned(0)
        gath(2, 3)
        inter(2, 0, 2)
        more()
        gath(3, 0)
        quant(2, 0, 2)
        routed(2)
        gath(3, 1, 2)
        inter(3, 0, 1)
        gath(3, 3)
        turned(1)
        quant(3, 0, 1)
        inter(3, 1, 2)
        quant(3, 1, 2)
        start1(3)
        for s in range(S):
            pass1(3, 3, codes[3][1], codes[3][2], 0, s)
        relu(3)
        hidden(0)
        hidden(1)
        xs = work.tile([P, S, 4 * T], BF16, name="gi", align_bytes=64, bufs=1)
        sc = keep.tile([P, S, T], U32, name="sc", align_bytes=64)
        ss = keep.tile([P, S, T], U8, name="ss", align_bytes=64)
        for s in range(S):
            interleave(pairs, xs, s, s + 1)
        for s in range(S):
            nc.vector.quantize_mx(out=sc[:, s, :].bitcast(FP8X4), scales=ss[:, s, :], in_=xs[:, s, :])
        for e in (2, 3):
            turned(e)
            hidden(e)
        results(0, 0, 1)
        results(2, 0, 1)
        for half in range(2):
            first(E + half, E, sc, ss, C * half)
        hsi = keep.tile([P, 4, 4 * P], BF16, name="hsi", align_bytes=64)
        for half in range(2):
            turn(E + half, hsi[:, 2 * half : 2 * half + 2, :])
        quantize_h(hsi[:], hc[:], hss[:])
        results(0, 2)
        results(2, 2)

        t1, t2 = [], []
        for n in range(NC):
            for r, ts in enumerate((t1, t2)):
                t = keep.tile([P, T], F32, name=f"t{r}{n}")
                nc.vector.tensor_tensor(t[:], y[n][:].indirect(pos_sb[r][:]), gt[:, r, n, :], MULT)
                ts.append(t)
        ysp = []
        for n in range(NC):
            ysp.append(pa.tile([P, T], F32, name="a"))
            layer2(E, ysp[n][:], n, hc[:], hss[:])
        t3 = [keep.tile([P, T], F32, name=f"t3{n}") for n in range(NC)]
        o = [keep.tile([P, T], F32, name=f"o{n}") for n in range(NC)]

        def plus_shared(n):
            nc.vector.tensor_tensor(t3[n][:], t1[n][:], ysp[n][:], ADD)

        def finish(n, c0, c1, engine):
            engine.tensor_tensor(o[n][:, c0:c1], t2[n][:, c0:c1], t3[n][:, c0:c1], ADD)
            nc.sync.dma_start(out=out[P * n : P * (n + 1), c0:c1], in_=o[n][:, c0:c1])

        plus_shared(0)
        finish(0, 0, T, nc.gpsimd)
        plus_shared(1)
        plus_shared(2)
        finish(1, 0, T, nc.vector)
        finish(2, 0, T // 2, nc.vector)
        finish(2, T // 2, T, nc.vector)
